import numpy as np, ml_dtypes
CORES = [2,34,66,98,130,162,194,226,258,290,322,354,386,418,450,482]
N = 16
R, TK = 32, 128
WID = [96,16,32,80,80,48,128,112,128,64,96,48,16,48,16,80]
def setup_inputs(rng):
    u = (rng.standard_normal((N, 128, R), dtype=np.float32) / 11).astype(ml_dtypes.bfloat16)
    return {"x": rng.standard_normal((N, 128, TK), dtype=np.float32).astype(ml_dtypes.bfloat16), "u": u, "ut": u.transpose(0, 2, 1).copy(), "vt": rng.standard_normal((N, R, 128), dtype=np.float32).astype(ml_dtypes.bfloat16)}
def setup_inputs_big(rng):
    d = setup_inputs(rng)
    for k in ("x", "u", "ut", "vt"): d[k] = (d[k].astype(np.float32) * 1024.0).astype(d[k].dtype)
    return d
def setup_inputs_small(rng):
    d = setup_inputs(rng)
    for k in ("x", "u", "ut", "vt"): d[k] = (d[k].astype(np.float32) * (1 / 1024.0)).astype(d[k].dtype)
    return d
def setup_inputs_apart(rng):
    d = setup_inputs(rng)
    f = (10.0 ** rng.permutation(np.linspace(-1.5, 1.5, N))).astype(np.float32).reshape(N, 1, 1)
    for k in ("x", "u", "ut", "vt"): d[k] = (d[k].astype(np.float32) * f).astype(d[k].dtype)
    return d
def tie_inputs(x):
    x = dict(x)
    x["ut"] = x["u"].transpose(0, 2, 1).copy()
    return x
def whole(x, u, ut, vt):
    X, U, VT = x.astype(np.float64), u.astype(np.float64), vt.astype(np.float64)
    y = np.stack([sum(VT[j].T @ (U[j].T @ X[r]) for j in range(N)) for r in range(N)])
    return {"y": y.astype(ml_dtypes.bfloat16 if x.dtype != np.float64 else np.float64)}
def reference(x, u, ut, vt):
    o = whole(x, u, ut, vt)["y"].copy()
    for r in range(N):
        o[r][:, WID[r]:] = np.nan
    return {"y": o}

@@ -1,0 +1,100 @@
+from concourse.bass import DstId, RemoteDMATransfer
+
+D = 128
+SCRATCH = {
+    "f_sb": ("sbuf", [128, 2 * D], "bfloat16"),
+    "x_sb": ("sbuf", [128, D], "bfloat16"),
+    "p_sb": ("sbuf", [128, D], "bfloat16"),
+    "r1": ("sbuf", [128, 3 * D], "bfloat16"),
+    "r2": ("sbuf", [128, 3 * D], "bfloat16"),
+    "y_sb": ("sbuf", [128, D], "bfloat16"),
+    "p_ps": ("psum", [128, 512], "float32"),
+    "y_ps": ("psum", [128, 512], "float32"),
+}
+SEMAPHORES = ["ld", "ldx", "mm1", "cp1", "arr1", "arr2", "snt", "mm2", "cp2", "st"]
+
+
+def _grid(cores, topo):
+    chips = sorted({topo.chip(c) for c in cores})
+    pos = {ch: i for i, ch in enumerate(chips)}
+
+    def cabled(a, b):
+        return topo.rack(topo.host(a)) != topo.rack(topo.host(b)) and topo.may_write(a, b) and topo.may_write(b, a)
+
+    cell, line = {}, {}
+    for c in cores:
+        pair = min(topo.host(d) for d in cores if topo.host(d) == topo.host(c) or cabled(c, d))
+        cell[c] = (pair, pos[topo.chip(c)] // 2)
+        line[c] = (topo.rack(topo.host(c)), pos[topo.chip(c)] % 2)
+    return cell, line
+
+
+def _send(g, core, topo, peers_of, srcs, land, sem, local_sem):
+    peers = peers_of(core)
+    mask = topo.mask(core, peers[0])
+    for d in peers:
+        mask &= topo.mask(core, d)
+    ids, dsts = [], []
+    for d in peers:
+        rid, pid = topo.addr(d, core)
+        ids.append(DstId(rid=rid, pnc=pid))
+        s = peers_of(d).index(core)
+        dsts.append(land[:, s * D:(s + 1) * D])
+    g.remote_dma_fused([RemoteDMATransfer(dst_ids=ids, dma_engine_mask=mask, remote_sem=sem, srcs=srcs, dsts=dsts,
+                                          alu_op=1 if len(srcs) > 1 else 0)], local_sem=local_sem)
+    return bin(mask).count("1")
+
+
+def rank_program(g, core, T, topo):
+    rank = T.rank_of(core)
+    if rank is None:
+        return
+    cores = list(T.cores)
+    W = T.tables["WID"][rank]
+    K = T.ut.shape[0]
+    cell, line = _grid(cores, topo)
+    S = T.sem
+
+    def cell_peers(c):
+        return [d for d in cores if cell[d] == cell[c] and d != c]
+
+    def line_peers(c):
+        return [d for d in cores if line[d] == line[c] and d != c]
+
+    ut, vt = T.f_sb[0:K, 0:D], T.f_sb[0:K, D:2 * D]
+    slots1 = [T.r1[:, s * D:(s + 1) * D] for s in range(3)]
+    slots2 = [T.r2[:, s * D:(s + 1) * D] for s in range(3)]
+
+    g.sync.dma_start(ut, T.ut[:, :]).then_inc(S.ld, 16)
+    g.scalar.dma_start(vt, T.vt[:, :]).then_inc(S.ld, 16)
+    g.scalar.dma_start(T.x_sb[:, 0:W], T.x[:, 0:W]).then_inc(S.ldx, 16)
+
+    g.tensor.wait_ge(S.ld, 32)
+    g.tensor.matmul(T.p_ps[:, 0:D], ut, vt, True, True).then_inc(S.mm1, 1)
+    g.vector.wait_ge(S.mm1, 1)
+    g.vector.tensor_copy(T.p_sb[:, :], T.p_ps[:, 0:D]).then_inc(S.cp1, 1)
+
+    g.wait_ge(S.cp1, 1)
+    e1 = _send(g, core, topo, cell_peers, [T.p_sb[:, :]], T.r1, S.arr1, S.snt)
+    g.wait_ge(S.arr1, 3 * e1)
+    e2 = _send(g, core, topo, line_peers, [T.p_sb[:, :]] + slots1, T.r2, S.arr2, S.snt)
+
+    x = T.x_sb[:, 0:W]
+    y = T.y_ps[:, 0:W]
+    g.tensor.wait_ge(S.cp1, 1)
+    g.tensor.wait_ge(S.ldx, 16)
+    g.tensor.matmul(y, T.p_sb[:, :], x, True, False)
+    g.tensor.wait_ge(S.arr1, 3 * e1)
+    for a in slots1:
+        g.tensor.matmul(y, a, x, False, False)
+    g.tensor.wait_ge(S.arr2, 3 * e2)
+    g.tensor.matmul(y, slots2[0], x, False, False)
+    g.tensor.matmul(y, slots2[1], x, False, False)
+    g.tensor.matmul(y, slots2[2], x, False, True).then_inc(S.mm2, 1)
+
+    g.vector.wait_ge(S.mm2, 1)
+    g.vector.tensor_copy(T.y_sb[:, 0:W], y).then_inc(S.cp2, 1)
+    g.sync.wait_ge(S.cp2, 1)
+    g.sync.dma_start(T.y[:, 0:W], T.y_sb[:, 0:W]).then_inc(S.st, 16)
+    g.sync.wait_ge(S.st, 16)
+    g.wait_ge(S.snt, e1 + e2)

@@ -1,17 +1,20 @@
 from concourse.bass import DstId, RemoteDMATransfer
+from concourse.mybir import AluOpType
 
 D = 128
 SCRATCH = {
     "f_sb": ("sbuf", [128, 2 * D], "bfloat16"),
     "x_sb": ("sbuf", [128, D], "bfloat16"),
     "p_sb": ("sbuf", [128, D], "bfloat16"),
-    "r1": ("sbuf", [128, 3 * D], "bfloat16"),
-    "r2": ("sbuf", [128, 3 * D], "bfloat16"),
+    "s_sb": ("sbuf", [128, D], "bfloat16"),
+    "r1": ("sbuf", [128, 4 * D], "bfloat16"),
+    "r2": ("sbuf", [128, 4 * D], "bfloat16"),
     "y_sb": ("sbuf", [128, D], "bfloat16"),
     "p_ps": ("psum", [128, 512], "float32"),
     "y_ps": ("psum", [128, 512], "float32"),
 }
-SEMAPHORES = ["ld", "ldx", "mm1", "cp1", "arr1", "arr2", "snt", "mm2", "cp2", "st"]
+SEMAPHORES = ["ld", "ldx", "mm1", "cp1", "add", "snt", "mm2", "cp2", "st"] + \
+             ["a1%d" % i for i in range(4)] + ["a2%d" % i for i in range(4)]
 
 
 def _grid(cores, topo):
@@ -29,22 +32,6 @@ def _grid(cores, topo):
     return cell, line
 
 
-def _send(g, core, topo, peers_of, srcs, land, sem, local_sem):
-    peers = peers_of(core)
-    mask = topo.mask(core, peers[0])
-    for d in peers:
-        mask &= topo.mask(core, d)
-    ids, dsts = [], []
-    for d in peers:
-        rid, pid = topo.addr(d, core)
-        ids.append(DstId(rid=rid, pnc=pid))
-        s = peers_of(d).index(core)
-        dsts.append(land[:, s * D:(s + 1) * D])
-    g.remote_dma_fused([RemoteDMATransfer(dst_ids=ids, dma_engine_mask=mask, remote_sem=sem, srcs=srcs, dsts=dsts,
-                                          alu_op=1 if len(srcs) > 1 else 0)], local_sem=local_sem)
-    return bin(mask).count("1")
-
-
 def rank_program(g, core, T, topo):
     rank = T.rank_of(core)
     if rank is None:
@@ -55,15 +42,29 @@ def rank_program(g, core, T, topo):
     cell, line = _grid(cores, topo)
     S = T.sem
 
-    def cell_peers(c):
-        return [d for d in cores if cell[d] == cell[c] and d != c]
+    def far(d):
+        return 0 if topo.same_plane(core, d) else (1 if topo.chip(core) == topo.chip(d) else 2)
 
-    def line_peers(c):
-        return [d for d in cores if line[d] == line[c] and d != c]
+    def gather(key, src, land, name):
+        group = [d for d in cores if key[d] == key[core]]
+        n, me = len(group), group.index(core)
+        peers = [d for d in group if d != core]
+        to = sorted(peers, key=lambda d: (far(d), (group.index(d) - me) % n))
+        frm = sorted(peers, key=lambda d: (far(d), (me - group.index(d)) % n))
+        mask = topo.mask(core, peers[0])
+        for d in peers:
+            mask &= topo.mask(core, d)
+        ids = []
+        for d in to:
+            rid, pid = topo.addr(d, core)
+            ids.append(DstId(rid=rid, pnc=pid))
+        g.remote_dma_fused([RemoteDMATransfer(dst_ids=ids, dma_engine_mask=mask, remote_sem=S[name % me], srcs=[src],
+                                              dsts=[land[:, me * D:(me + 1) * D]] * len(to), alu_op=0)],
+                           local_sem=S.snt)
+        e = bin(mask).count("1")
+        return e, [(S[name % group.index(d)], e, land[:, group.index(d) * D:(group.index(d) + 1) * D]) for d in frm]
 
     ut, vt = T.f_sb[0:K, 0:D], T.f_sb[0:K, D:2 * D]
-    slots1 = [T.r1[:, s * D:(s + 1) * D] for s in range(3)]
-    slots2 = [T.r2[:, s * D:(s + 1) * D] for s in range(3)]
 
     g.sync.dma_start(ut, T.ut[:, :]).then_inc(S.ld, 16)
     g.scalar.dma_start(vt, T.vt[:, :]).then_inc(S.ld, 16)
@@ -75,22 +76,29 @@ def rank_program(g, core, T, topo):
     g.vector.tensor_copy(T.p_sb[:, :], T.p_ps[:, 0:D]).then_inc(S.cp1, 1)
 
     g.wait_ge(S.cp1, 1)
-    e1 = _send(g, core, topo, cell_peers, [T.p_sb[:, :]], T.r1, S.arr1, S.snt)
-    g.wait_ge(S.arr1, 3 * e1)
-    e2 = _send(g, core, topo, line_peers, [T.p_sb[:, :]] + slots1, T.r2, S.arr2, S.snt)
+    e1, in1 = gather(cell, T.p_sb[:, :], T.r1, "a1%d")
+
+    for i, (sem, n, slot) in enumerate(in1):
+        g.vector.wait_ge(sem, n)
+        if i:
+            g.vector.wait_ge(S.add, i)
+        out = T.s_sb[:, :] if i == len(in1) - 1 else T.p_ps[:, (i + 1) * D:(i + 2) * D]
+        g.vector.tensor_tensor(out, T.p_ps[:, i * D:(i + 1) * D], slot, AluOpType.add).then_inc(S.add, 1)
+
+    g.wait_ge(S.add, len(in1))
+    e2, in2 = gather(line, T.s_sb[:, :], T.r2, "a2%d")
 
     x = T.x_sb[:, 0:W]
     y = T.y_ps[:, 0:W]
-    g.tensor.wait_ge(S.cp1, 1)
+    g.tensor.wait_ge(S.add, len(in1))
     g.tensor.wait_ge(S.ldx, 16)
-    g.tensor.matmul(y, T.p_sb[:, :], x, True, False)
-    g.tensor.wait_ge(S.arr1, 3 * e1)
-    for a in slots1:
-        g.tensor.matmul(y, a, x, False, False)
-    g.tensor.wait_ge(S.arr2, 3 * e2)
-    g.tensor.matmul(y, slots2[0], x, False, False)
-    g.tensor.matmul(y, slots2[1], x, False, False)
-    g.tensor.matmul(y, slots2[2], x, False, True).then_inc(S.mm2, 1)
+    g.tensor.matmul(y, T.s_sb[:, :], x, True, False)
+    for i, (sem, n, slot) in enumerate(in2):
+        g.tensor.wait_ge(sem, n)
+        if i == len(in2) - 1:
+            g.tensor.matmul(y, slot, x, False, True).then_inc(S.mm2, 1)
+        else:
+            g.tensor.matmul(y, slot, x, False, False)
 
     g.vector.wait_ge(S.mm2, 1)
     g.vector.tensor_copy(T.y_sb[:, 0:W], y).then_inc(S.cp2, 1)

@@ -1,35 +1,19 @@
 from concourse.bass import DstId, RemoteDMATransfer
-from concourse.mybir import AluOpType
 
 D = 128
+G = 8
 SCRATCH = {
-    "f_sb": ("sbuf", [128, 2 * D], "bfloat16"),
+    "da": ("dram", [G * 128, 64], "bfloat16"),
+    "db": ("dram", [G * 128, 64], "bfloat16"),
+    "fa": ("sbuf", [128, G * 64], "bfloat16"),
+    "fb": ("sbuf", [128, G * 64], "bfloat16"),
     "x_sb": ("sbuf", [128, D], "bfloat16"),
-    "p_sb": ("sbuf", [128, D], "bfloat16"),
-    "s_sb": ("sbuf", [128, D], "bfloat16"),
-    "r1": ("sbuf", [128, 4 * D], "bfloat16"),
-    "r2": ("sbuf", [128, 4 * D], "bfloat16"),
+    "a_sb": ("sbuf", [128, D], "bfloat16"),
     "y_sb": ("sbuf", [128, D], "bfloat16"),
-    "p_ps": ("psum", [128, 512], "float32"),
+    "a_ps": ("psum", [128, 512], "float32"),
     "y_ps": ("psum", [128, 512], "float32"),
 }
-SEMAPHORES = ["ld", "ldx", "mm1", "cp1", "add", "snt", "mm2", "cp2", "st"] + \
-             ["a1%d" % i for i in range(4)] + ["a2%d" % i for i in range(4)]
-
-
-def _grid(cores, topo):
-    chips = sorted({topo.chip(c) for c in cores})
-    pos = {ch: i for i, ch in enumerate(chips)}
-
-    def cabled(a, b):
-        return topo.rack(topo.host(a)) != topo.rack(topo.host(b)) and topo.may_write(a, b) and topo.may_write(b, a)
-
-    cell, line = {}, {}
-    for c in cores:
-        pair = min(topo.host(d) for d in cores if topo.host(d) == topo.host(c) or cabled(c, d))
-        cell[c] = (pair, pos[topo.chip(c)] // 2)
-        line[c] = (topo.rack(topo.host(c)), pos[topo.chip(c)] % 2)
-    return cell, line
+SEMAPHORES = ["ld", "ldx", "ap", "a1", "ad", "ln1", "ln2", "mm1", "cp1", "snt", "mm2", "cp2", "st"]
 
 
 def rank_program(g, core, T, topo):
@@ -38,71 +22,78 @@ def rank_program(g, core, T, topo):
         return
     cores = list(T.cores)
     W = T.tables["WID"][rank]
-    K = T.ut.shape[0]
-    cell, line = _grid(cores, topo)
     S = T.sem
+    H = D // 2
 
-    def far(d):
-        return 0 if topo.same_plane(core, d) else (1 if topo.chip(core) == topo.chip(d) else 2)
+    def rk(c):
+        return topo.rack(topo.host(c))
 
-    def gather(key, src, land, name):
-        group = [d for d in cores if key[d] == key[core]]
-        n, me = len(group), group.index(core)
-        peers = [d for d in group if d != core]
-        to = sorted(peers, key=lambda d: (far(d), (group.index(d) - me) % n))
-        frm = sorted(peers, key=lambda d: (far(d), (me - group.index(d)) % n))
-        mask = topo.mask(core, peers[0])
-        for d in peers:
-            mask &= topo.mask(core, d)
-        ids = []
-        for d in to:
-            rid, pid = topo.addr(d, core)
-            ids.append(DstId(rid=rid, pnc=pid))
-        g.remote_dma_fused([RemoteDMATransfer(dst_ids=ids, dma_engine_mask=mask, remote_sem=S[name % me], srcs=[src],
-                                              dsts=[land[:, me * D:(me + 1) * D]] * len(to), alu_op=0)],
-                           local_sem=S.snt)
-        e = bin(mask).count("1")
-        return e, [(S[name % group.index(d)], e, land[:, group.index(d) * D:(group.index(d) + 1) * D]) for d in frm]
+    def place(c):
+        return [d for d in cores if rk(d) == rk(c)].index(c)
 
-    ut, vt = T.f_sb[0:K, 0:D], T.f_sb[0:K, D:2 * D]
+    rack = [d for d in cores if rk(d) == rk(core)]
+    nr, me = len(rack), place(core)
+    rest = [rack[(me + i) % nr] for i in range(1, nr)]
+    partner = [d for d in cores if rk(d) != rk(core) and topo.chip(d) == topo.chip(core)
+               and topo.may_write(core, d) and topo.may_write(d, core)][0]
 
-    g.sync.dma_start(ut, T.ut[:, :]).then_inc(S.ld, 16)
-    g.scalar.dma_start(vt, T.vt[:, :]).then_inc(S.ld, 16)
+    mask = topo.mask(core, partner)
+    for d in rest:
+        mask &= topo.mask(core, d)
+    E = bin(mask).count("1")
+
+    def slot(t, i):
+        return t[i * 128:(i + 1) * 128, :]
+
+    ids = []
+    for d in rest:
+        rid, pid = topo.addr(d, core)
+        ids.append(DstId(rid=rid, pnc=pid))
+
+    def spread(piece, sem):
+        g.remote_dma_fused([RemoteDMATransfer(dst_ids=ids, dma_engine_mask=mask, remote_sem=sem, srcs=[piece],
+                                              dsts=[piece] * len(rest), alu_op=0)], local_sem=S.snt)
+
+    lo = me * 128
+    for q, src, a in ((g.sync, T.ut, 0), (g.scalar, T.vt, 2)):
+        q.dma_start(T.da[lo + a:lo + 128:4, :], src[:, 0:H]).then_inc(S.ld, 16)
+        q.dma_start(T.da[lo + a + 1:lo + 128:4, :], src[:, H:D]).then_inc(S.ld, 16)
     g.scalar.dma_start(T.x_sb[:, 0:W], T.x[:, 0:W]).then_inc(S.ldx, 16)
 
-    g.tensor.wait_ge(S.ld, 32)
-    g.tensor.matmul(T.p_ps[:, 0:D], ut, vt, True, True).then_inc(S.mm1, 1)
+    g.wait_ge(S.ld, 64)
+    rid, pid = topo.addr(partner, core)
+    g.remote_dma(slot(T.db, place(partner)), slot(T.da, me), S.ap, S.snt, pid, rid, mask)
+    spread(slot(T.da, me), S.a1)
+    g.wait_ge(S.ap, E)
+    spread(slot(T.db, me), S.ad)
+
+    g.sync.wait_ge(S.ld, 64)
+    g.sync.wait_ge(S.a1, E * len(rest))
+    g.sync.dma_start(T.fa[:, :], T.da[:, :]).then_inc(S.ln1, 16)
+    g.scalar.wait_ge(S.ap, E)
+    g.scalar.wait_ge(S.ad, E * len(rest))
+    g.scalar.dma_start(T.fb[:, :], T.db[:, :]).then_inc(S.ln2, 16)
+
+    A = T.a_ps[:, 0:D]
+    nb = G * 64 // (2 * D)
+    for i, (f, sem) in enumerate(((T.fa, S.ln1), (T.fb, S.ln2))):
+        g.tensor.wait_ge(sem, 16)
+        for b in range(nb):
+            c = 2 * D * b
+            if i == 1 and b == nb - 1:
+                g.tensor.matmul(A, f[:, c:c + D], f[:, c + D:c + 2 * D], False, True).then_inc(S.mm1, 1)
+            else:
+                g.tensor.matmul(A, f[:, c:c + D], f[:, c + D:c + 2 * D], i == 0 and b == 0, False)
     g.vector.wait_ge(S.mm1, 1)
-    g.vector.tensor_copy(T.p_sb[:, :], T.p_ps[:, 0:D]).then_inc(S.cp1, 1)
+    g.vector.tensor_copy(T.a_sb[:, :], A).then_inc(S.cp1, 1)
 
-    g.wait_ge(S.cp1, 1)
-    e1, in1 = gather(cell, T.p_sb[:, :], T.r1, "a1%d")
-
-    for i, (sem, n, slot) in enumerate(in1):
-        g.vector.wait_ge(sem, n)
-        if i:
-            g.vector.wait_ge(S.add, i)
-        out = T.s_sb[:, :] if i == len(in1) - 1 else T.p_ps[:, (i + 1) * D:(i + 2) * D]
-        g.vector.tensor_tensor(out, T.p_ps[:, i * D:(i + 1) * D], slot, AluOpType.add).then_inc(S.add, 1)
-
-    g.wait_ge(S.add, len(in1))
-    e2, in2 = gather(line, T.s_sb[:, :], T.r2, "a2%d")
-
-    x = T.x_sb[:, 0:W]
     y = T.y_ps[:, 0:W]
-    g.tensor.wait_ge(S.add, len(in1))
+    g.tensor.wait_ge(S.cp1, 1)
     g.tensor.wait_ge(S.ldx, 16)
-    g.tensor.matmul(y, T.s_sb[:, :], x, True, False)
-    for i, (sem, n, slot) in enumerate(in2):
-        g.tensor.wait_ge(sem, n)
-        if i == len(in2) - 1:
-            g.tensor.matmul(y, slot, x, False, True).then_inc(S.mm2, 1)
-        else:
-            g.tensor.matmul(y, slot, x, False, False)
-
+    g.tensor.matmul(y, T.a_sb[:, :], T.x_sb[:, 0:W], True, True).then_inc(S.mm2, 1)
     g.vector.wait_ge(S.mm2, 1)
     g.vector.tensor_copy(T.y_sb[:, 0:W], y).then_inc(S.cp2, 1)
     g.sync.wait_ge(S.cp2, 1)
     g.sync.dma_start(T.y[:, 0:W], T.y_sb[:, 0:W]).then_inc(S.st, 16)
     g.sync.wait_ge(S.st, 16)
-    g.wait_ge(S.snt, e1 + e2)
+    g.wait_ge(S.snt, 3 * E)

@@ -13,7 +13,8 @@ SCRATCH = {
     "a_ps": ("psum", [128, 512], "float32"),
     "y_ps": ("psum", [128, 512], "float32"),
 }
-SEMAPHORES = ["ld", "ldx", "ap", "a1", "ad", "ln1", "ln2", "mm1", "cp1", "snt", "mm2", "cp2", "st"]
+SEMAPHORES = ["ld", "ldx", "ap", "a1", "ln1", "lnA", "ln2", "mm1", "cp1", "snt", "mm2", "cp2", "st"] + \
+             ["ad%d" % i for i in range(G)]
 
 
 def rank_program(g, core, T, topo):
@@ -28,11 +29,8 @@ def rank_program(g, core, T, topo):
     def rk(c):
         return topo.rack(topo.host(c))
 
-    def place(c):
-        return [d for d in cores if rk(d) == rk(c)].index(c)
-
     rack = [d for d in cores if rk(d) == rk(core)]
-    nr, me = len(rack), place(core)
+    nr, me = len(rack), rack.index(core)
     rest = [rack[(me + i) % nr] for i in range(1, nr)]
     partner = [d for d in cores if rk(d) != rk(core) and topo.chip(d) == topo.chip(core)
                and topo.may_write(core, d) and topo.may_write(d, core)][0]
@@ -40,50 +38,62 @@ def rank_program(g, core, T, topo):
     mask = topo.mask(core, partner)
     for d in rest:
         mask &= topo.mask(core, d)
-    E = bin(mask).count("1")
+    bits = [1 << b for b in range(16) if (mask >> b) & 1]
+    E = len(bits)
+    EC = 2
+    cmask = bits[0] | bits[1]
 
-    def slot(t, i):
-        return t[i * 128:(i + 1) * 128, :]
+    def slots(t, i, n=1):
+        return t[i * 128:(i + n) * 128, :]
+
+    def came(i):
+        return S["ad%d" % ((me - i) % nr)]
 
     ids = []
     for d in rest:
         rid, pid = topo.addr(d, core)
         ids.append(DstId(rid=rid, pnc=pid))
 
-    def spread(piece, sem):
-        g.remote_dma_fused([RemoteDMATransfer(dst_ids=ids, dma_engine_mask=mask, remote_sem=sem, srcs=[piece],
-                                              dsts=[piece] * len(rest), alu_op=0)], local_sem=S.snt)
+    def spread(t, sem):
+        g.remote_dma_fused([RemoteDMATransfer(dst_ids=ids, dma_engine_mask=mask, remote_sem=sem, srcs=[slots(t, 0)],
+                                              dsts=[slots(t, i) for i in range(1, nr)], alu_op=0)], local_sem=S.snt)
 
-    lo = me * 128
     for q, src, a in ((g.sync, T.ut, 0), (g.scalar, T.vt, 2)):
-        q.dma_start(T.da[lo + a:lo + 128:4, :], src[:, 0:H]).then_inc(S.ld, 16)
-        q.dma_start(T.da[lo + a + 1:lo + 128:4, :], src[:, H:D]).then_inc(S.ld, 16)
+        q.dma_start(T.da[a:128:4, :], src[:, 0:H]).then_inc(S.ld, 16)
+        q.dma_start(T.da[a + 1:128:4, :], src[:, H:D]).then_inc(S.ld, 16)
     g.scalar.dma_start(T.x_sb[:, 0:W], T.x[:, 0:W]).then_inc(S.ldx, 16)
 
     g.wait_ge(S.ld, 64)
     rid, pid = topo.addr(partner, core)
-    g.remote_dma(slot(T.db, place(partner)), slot(T.da, me), S.ap, S.snt, pid, rid, mask)
-    spread(slot(T.da, me), S.a1)
-    g.wait_ge(S.ap, E)
-    spread(slot(T.db, me), S.ad)
+    g.remote_dma(slots(T.db, 0), slots(T.da, 0), S.ap, S.snt, pid, rid, cmask)
+    spread(T.da, S.a1)
+    g.wait_ge(S.ap, EC)
+    spread(T.db, S["ad%d" % me])
 
+    B2 = T.fb[:, 2 * D:4 * D]
     g.sync.wait_ge(S.ld, 64)
     g.sync.wait_ge(S.a1, E * len(rest))
     g.sync.dma_start(T.fa[:, :], T.da[:, :]).then_inc(S.ln1, 16)
-    g.scalar.wait_ge(S.ap, E)
-    g.scalar.wait_ge(S.ad, E * len(rest))
-    g.scalar.dma_start(T.fb[:, :], T.db[:, :]).then_inc(S.ln2, 16)
+    g.scalar.wait_ge(S.ap, EC)
+    for i in (1, 2, 3):
+        g.scalar.wait_ge(came(i), E)
+    g.scalar.dma_start(T.fb[:, 0:2 * D], slots(T.db, 0, 4)).then_inc(S.lnA, 16)
+    for i in (4, 5):
+        g.scalar.wait_ge(came(i), E)
+    g.scalar.dma_start(T.fb[0:64, 2 * D:4 * D], slots(T.db, 4, 2)).then_inc(S.ln2, 16)
+    g.sync.wait_ge(came(6), E)
+    g.sync.dma_start(T.fb[64:96, 2 * D:4 * D], slots(T.db, 6)).then_inc(S.ln2, 16)
+    g.scalar.wait_ge(came(7), E)
+    g.scalar.dma_start(T.fb[96:128, 2 * D:4 * D], slots(T.db, 7)).then_inc(S.ln2, 16)
 
     A = T.a_ps[:, 0:D]
-    nb = G * 64 // (2 * D)
-    for i, (f, sem) in enumerate(((T.fa, S.ln1), (T.fb, S.ln2))):
-        g.tensor.wait_ge(sem, 16)
-        for b in range(nb):
-            c = 2 * D * b
-            if i == 1 and b == nb - 1:
-                g.tensor.matmul(A, f[:, c:c + D], f[:, c + D:c + 2 * D], False, True).then_inc(S.mm1, 1)
-            else:
-                g.tensor.matmul(A, f[:, c:c + D], f[:, c + D:c + 2 * D], i == 0 and b == 0, False)
+    g.tensor.wait_ge(S.ln1, 16)
+    g.tensor.matmul(A, T.fa[:, 0:D], T.fa[:, D:2 * D], True, False)
+    g.tensor.matmul(A, T.fa[:, 2 * D:3 * D], T.fa[:, 3 * D:4 * D], False, False)
+    g.tensor.wait_ge(S.lnA, 16)
+    g.tensor.matmul(A, T.fb[:, 0:D], T.fb[:, D:2 * D], False, False)
+    g.tensor.wait_ge(S.ln2, 48)
+    g.tensor.matmul(A, T.fb[:, 2 * D:3 * D], T.fb[:, 3 * D:4 * D], False, True).then_inc(S.mm1, 1)
     g.vector.wait_ge(S.mm1, 1)
     g.vector.tensor_copy(T.a_sb[:, :], A).then_inc(S.cp1, 1)
 
@@ -96,4 +106,4 @@ def rank_program(g, core, T, topo):
     g.sync.wait_ge(S.cp2, 1)
     g.sync.dma_start(T.y[:, 0:W], T.y_sb[:, 0:W]).then_inc(S.st, 16)
     g.sync.wait_ge(S.st, 16)
-    g.wait_ge(S.snt, 3 * E)
+    g.wait_ge(S.snt, EC + 2 * E)

from concourse.bass import DstId, RemoteDMATransfer

D = 128
G = 8
SCRATCH = {
    "da": ("dram", [G * 128, 64], "bfloat16"),
    "db": ("dram", [G * 128, 64], "bfloat16"),
    "fa": ("sbuf", [128, G * 64], "bfloat16"),
    "fb": ("sbuf", [128, G * 64], "bfloat16"),
    "x_sb": ("sbuf", [128, D], "bfloat16"),
    "a_sb": ("sbuf", [128, D], "bfloat16"),
    "y_sb": ("sbuf", [128, D], "bfloat16"),
    "a_ps": ("psum", [128, 512], "float32"),
    "y_ps": ("psum", [128, 512], "float32"),
}
SEMAPHORES = ["ld", "ldx", "ap", "a1", "ln1", "lnA", "ln2", "mm1", "cp1", "snt", "mm2", "cp2", "st"] + \
             ["ad%d" % i for i in range(G)]


def rank_program(g, core, T, topo):
    rank = T.rank_of(core)
    if rank is None:
        return
    cores = list(T.cores)
    W = T.tables["WID"][rank]
    S = T.sem
    H = D // 2

    def rk(c):
        return topo.rack(topo.host(c))

    rack = [d for d in cores if rk(d) == rk(core)]
    nr, me = len(rack), rack.index(core)
    rest = [rack[(me + i) % nr] for i in range(1, nr)]
    partner = [d for d in cores if rk(d) != rk(core) and topo.chip(d) == topo.chip(core)
               and topo.may_write(core, d) and topo.may_write(d, core)][0]

    mask = topo.mask(core, partner)
    for d in rest:
        mask &= topo.mask(core, d)
    bits = [1 << b for b in range(16) if (mask >> b) & 1]
    E = len(bits)
    EC = 2
    cmask = bits[0] | bits[1]

    def slots(t, i, n=1):
        return t[i * 128:(i + n) * 128, :]

    def came(i):
        return S["ad%d" % ((me - i) % nr)]

    ids = []
    for d in rest:
        rid, pid = topo.addr(d, core)
        ids.append(DstId(rid=rid, pnc=pid))

    def spread(t, sem):
        g.remote_dma_fused([RemoteDMATransfer(dst_ids=ids, dma_engine_mask=mask, remote_sem=sem, srcs=[slots(t, 0)],
                                              dsts=[slots(t, i) for i in range(1, nr)], alu_op=0)], local_sem=S.snt)

    for q, src, a in ((g.sync, T.ut, 0), (g.scalar, T.vt, 2)):
        q.dma_start(T.da[a:128:4, :], src[:, 0:H]).then_inc(S.ld, 16)
        q.dma_start(T.da[a + 1:128:4, :], src[:, H:D]).then_inc(S.ld, 16)
    g.scalar.dma_start(T.x_sb[:, 0:W], T.x[:, 0:W]).then_inc(S.ldx, 16)

    g.wait_ge(S.ld, 64)
    rid, pid = topo.addr(partner, core)
    g.remote_dma(slots(T.db, 0), slots(T.da, 0), S.ap, S.snt, pid, rid, cmask)
    spread(T.da, S.a1)
    g.wait_ge(S.ap, EC)
    spread(T.db, S["ad%d" % me])

    B2 = T.fb[:, 2 * D:4 * D]
    g.sync.wait_ge(S.ld, 64)
    g.sync.wait_ge(S.a1, E * len(rest))
    g.sync.dma_start(T.fa[:, :], T.da[:, :]).then_inc(S.ln1, 16)
    g.scalar.wait_ge(S.ap, EC)
    for i in (1, 2, 3):
        g.scalar.wait_ge(came(i), E)
    g.scalar.dma_start(T.fb[:, 0:2 * D], slots(T.db, 0, 4)).then_inc(S.lnA, 16)
    for i in (4, 5):
        g.scalar.wait_ge(came(i), E)
    g.scalar.dma_start(T.fb[0:64, 2 * D:4 * D], slots(T.db, 4, 2)).then_inc(S.ln2, 16)
    g.sync.wait_ge(came(6), E)
    g.sync.dma_start(T.fb[64:96, 2 * D:4 * D], slots(T.db, 6)).then_inc(S.ln2, 16)
    g.scalar.wait_ge(came(7), E)
    g.scalar.dma_start(T.fb[96:128, 2 * D:4 * D], slots(T.db, 7)).then_inc(S.ln2, 16)

    A = T.a_ps[:, 0:D]
    g.tensor.wait_ge(S.ln1, 16)
    g.tensor.matmul(A, T.fa[:, 0:D], T.fa[:, D:2 * D], True, False)
    g.tensor.matmul(A, T.fa[:, 2 * D:3 * D], T.fa[:, 3 * D:4 * D], False, False)
    g.tensor.wait_ge(S.lnA, 16)
    g.tensor.matmul(A, T.fb[:, 0:D], T.fb[:, D:2 * D], False, False)
    g.tensor.wait_ge(S.ln2, 48)
    g.tensor.matmul(A, T.fb[:, 2 * D:3 * D], T.fb[:, 3 * D:4 * D], False, True).then_inc(S.mm1, 1)
    g.vector.wait_ge(S.mm1, 1)
    g.vector.tensor_copy(T.a_sb[:, :], A).then_inc(S.cp1, 1)

    y = T.y_ps[:, 0:W]
    g.tensor.wait_ge(S.cp1, 1)
    g.tensor.wait_ge(S.ldx, 16)
    g.tensor.matmul(y, T.a_sb[:, :], T.x_sb[:, 0:W], True, True).then_inc(S.mm2, 1)
    g.vector.wait_ge(S.mm2, 1)
    g.vector.tensor_copy(T.y_sb[:, 0:W], y).then_inc(S.cp2, 1)
    g.sync.wait_ge(S.cp2, 1)
    g.sync.dma_start(T.y[:, 0:W], T.y_sb[:, 0:W]).then_inc(S.st, 16)
    g.sync.wait_ge(S.st, 16)
    g.wait_ge(S.snt, EC + 2 * E)
